import numpy as np
import ml_dtypes

BF16 = ml_dtypes.bfloat16


def bf(x):
    return np.asarray(x, np.float32).astype(BF16)


def f32(x):
    return np.asarray(x, np.float32)


def f64(x):
    return np.asarray(x).astype(np.float64)


def striped(idx):
    return np.tile(idx.reshape(-1, 16).T, (8, 1))


def rows(idx, k):
    return np.tile(idx, (k, 1))


def look(tab, idx):
    return np.take_along_axis(f64(tab), rows(idx, len(tab)), axis=1)


K, S, V, N = 256, 2048, 512, 512


def silu(v):
    return v / (1.0 + np.exp(-v))


def setup_inputs():
    return {"tab": f32(np.random.standard_normal((2, K, S))), "y": f32(np.random.standard_normal((K, V))), "offs": striped(np.random.permutation(S)[:N])}


def reference(tab, y, offs):
    idx = offs[:16].T.reshape(-1)
    x = (np.maximum(look(tab[0], idx), f64(y))) * (silu(look(tab[1], idx)))
    return x

@@ -1,0 +1,34 @@
+import concourse.mybir as mybir
+
+F32, U16 = mybir.dt.float32, mybir.dt.uint16
+ALU = mybir.AluOpType
+SILU = mybir.ActivationFunctionType.Silu
+P = 128
+
+
+def tile_lookup_vg_maxsilu_out_kernel(tc, tab, y, offs, out):
+    nc = tc.nc
+    rows, places = tab.shape[1], tab.shape[2]
+    picks = y.shape[1]
+    blocks = rows // P
+
+    with tc.tile_pool(name="held", bufs=1) as held, tc.tile_pool(name="block", bufs=blocks) as block_pool:
+        offsets = held.tile([P, picks // 16], U16, name="offsets")
+        nc.sync.dma_start(offsets[:], offs)
+
+        for b in range(blocks):
+            block_rows = slice(b * P, (b + 1) * P)
+            values = block_pool.tile([P, places], F32, name="values")
+            gates = block_pool.tile([P, places], F32, name="gates")
+            stream = block_pool.tile([P, picks], F32, name="stream")
+            nc.sync.dma_start(values[:], tab[0, block_rows, :])
+            nc.sync.dma_start(stream[:], y[block_rows, :])
+            nc.sync.dma_start(gates[:], tab[1, block_rows, :])
+
+            larger = block_pool.tile([P, picks], F32, name="larger")
+            gated = block_pool.tile([P, picks], F32, name="gated")
+            product = block_pool.tile([P, picks], F32, name="product")
+            nc.vector.tensor_tensor(larger[:], values[:].indirect(offsets[:]), stream[:], ALU.max)
+            nc.scalar.activation(gated[:], gates[:].indirect(offsets[:]), SILU)
+            nc.vector.tensor_tensor(product[:], larger[:], gated[:], ALU.mult)
+            nc.sync.dma_start(out[block_rows, :], product[:])

@@ -4,6 +4,8 @@ F32, U16 = mybir.dt.float32, mybir.dt.uint16
 ALU = mybir.AluOpType
 SILU = mybir.ActivationFunctionType.Silu
 P = 128
+GROUP = 16
+HALVES = 2
 
 
 def tile_lookup_vg_maxsilu_out_kernel(tc, tab, y, offs, out):
@@ -11,24 +13,35 @@ def tile_lookup_vg_maxsilu_out_kernel(tc, tab, y, offs, out):
     rows, places = tab.shape[1], tab.shape[2]
     picks = y.shape[1]
     blocks = rows // P
+    half = picks // HALVES
 
-    with tc.tile_pool(name="held", bufs=1) as held, tc.tile_pool(name="block", bufs=blocks) as block_pool:
-        offsets = held.tile([P, picks // 16], U16, name="offsets")
+    with tc.tile_pool(name="held", bufs=1) as held:
+        offsets = held.tile([P, picks // GROUP], U16, name="offsets")
         nc.sync.dma_start(offsets[:], offs)
+
+        gates, values, streams = [], [], []
+        for b in range(blocks):
+            block_rows = slice(b * P, (b + 1) * P)
+            gates.append(held.tile([P, places], F32, name=f"gates{b}"))
+            values.append(held.tile([P, places], F32, name=f"values{b}"))
+            streams.append(held.tile([P, picks], F32, name=f"stream{b}"))
+            nc.sync.dma_start(gates[b][:], tab[1, block_rows, :])
+            nc.sync.dma_start(values[b][:], tab[0, block_rows, :])
+            for h in range(HALVES):
+                cols = slice(h * half, (h + 1) * half)
+                nc.sync.dma_start(streams[b][:, cols], y[block_rows, cols])
 
         for b in range(blocks):
             block_rows = slice(b * P, (b + 1) * P)
-            values = block_pool.tile([P, places], F32, name="values")
-            gates = block_pool.tile([P, places], F32, name="gates")
-            stream = block_pool.tile([P, picks], F32, name="stream")
-            nc.sync.dma_start(values[:], tab[0, block_rows, :])
-            nc.sync.dma_start(stream[:], y[block_rows, :])
-            nc.sync.dma_start(gates[:], tab[1, block_rows, :])
-
-            larger = block_pool.tile([P, picks], F32, name="larger")
-            gated = block_pool.tile([P, picks], F32, name="gated")
-            product = block_pool.tile([P, picks], F32, name="product")
-            nc.vector.tensor_tensor(larger[:], values[:].indirect(offsets[:]), stream[:], ALU.max)
-            nc.scalar.activation(gated[:], gates[:].indirect(offsets[:]), SILU)
-            nc.vector.tensor_tensor(product[:], larger[:], gated[:], ALU.mult)
-            nc.sync.dma_start(out[block_rows, :], product[:])
+            gated = held.tile([P, picks], F32, name=f"gated{b}")
+            larger = held.tile([P, picks], F32, name=f"larger{b}")
+            product = held.tile([P, picks], F32, name=f"product{b}")
+            nc.scalar.activation(gated[:], gates[b][:].indirect(offsets[:]), SILU)
+            for h in range(HALVES):
+                cols = slice(h * half, (h + 1) * half)
+                half_list = offsets[:, h * half // GROUP : (h + 1) * half // GROUP]
+                nc.vector.tensor_tensor(larger[:, cols], values[b][:].indirect(half_list), streams[b][:, cols], ALU.max)
+            for h in range(HALVES):
+                cols = slice(h * half, (h + 1) * half)
+                nc.vector.tensor_tensor(product[:, cols], larger[:, cols], gated[:, cols], ALU.mult)
+                nc.sync.dma_start(out[block_rows, cols], product[:, cols])

@@ -17,7 +17,6 @@ def tile_lookup_vg_maxsilu_out_kernel(tc, tab, y, offs, out):
 
     with tc.tile_pool(name="held", bufs=1) as held:
         offsets = held.tile([P, picks // GROUP], U16, name="offsets")
-        nc.sync.dma_start(offsets[:], offs)
 
         gates, values, streams = [], [], []
         for b in range(blocks):
@@ -26,10 +25,10 @@ def tile_lookup_vg_maxsilu_out_kernel(tc, tab, y, offs, out):
             values.append(held.tile([P, places], F32, name=f"values{b}"))
             streams.append(held.tile([P, picks], F32, name=f"stream{b}"))
             nc.sync.dma_start(gates[b][:], tab[1, block_rows, :])
+            if b == 0:
+                nc.sync.dma_start(offsets[:], offs)
+            nc.sync.dma_start(streams[b][:], y[block_rows, :])
             nc.sync.dma_start(values[b][:], tab[0, block_rows, :])
-            for h in range(HALVES):
-                cols = slice(h * half, (h + 1) * half)
-                nc.sync.dma_start(streams[b][:, cols], y[block_rows, cols])
 
         for b in range(blocks):
             block_rows = slice(b * P, (b + 1) * P)

@@ -6,6 +6,7 @@ SILU = mybir.ActivationFunctionType.Silu
 P = 128
 GROUP = 16
 HALVES = 2
+QUARTERS = 4
 
 
 def tile_lookup_vg_maxsilu_out_kernel(tc, tab, y, offs, out):
@@ -13,7 +14,7 @@ def tile_lookup_vg_maxsilu_out_kernel(tc, tab, y, offs, out):
     rows, places = tab.shape[1], tab.shape[2]
     picks = y.shape[1]
     blocks = rows // P
-    half = picks // HALVES
+    half, quarter = picks // HALVES, picks // QUARTERS
 
     with tc.tile_pool(name="held", bufs=1) as held:
         offsets = held.tile([P, picks // GROUP], U16, name="offsets")
@@ -23,23 +24,24 @@ def tile_lookup_vg_maxsilu_out_kernel(tc, tab, y, offs, out):
             block_rows = slice(b * P, (b + 1) * P)
             gates.append(held.tile([P, places], F32, name=f"gates{b}"))
             values.append(held.tile([P, places], F32, name=f"values{b}"))
-            streams.append(held.tile([P, picks], F32, name=f"stream{b}"))
+            streams.append(held.tile([P, picks + quarter], F32, name=f"stream{b}"))
             nc.sync.dma_start(gates[b][:], tab[1, block_rows, :])
             if b == 0:
                 nc.sync.dma_start(offsets[:], offs)
-            nc.sync.dma_start(streams[b][:], y[block_rows, :])
+            nc.sync.dma_start(streams[b][:, :half], y[block_rows, :half])
             nc.sync.dma_start(values[b][:], tab[0, block_rows, :])
+            nc.sync.dma_start(streams[b][:, half:picks], y[block_rows, half:])
 
         for b in range(blocks):
             block_rows = slice(b * P, (b + 1) * P)
             gated = held.tile([P, picks], F32, name=f"gated{b}")
             larger = held.tile([P, picks], F32, name=f"larger{b}")
-            product = held.tile([P, picks], F32, name=f"product{b}")
             nc.scalar.activation(gated[:], gates[b][:].indirect(offsets[:]), SILU)
-            for h in range(HALVES):
-                cols = slice(h * half, (h + 1) * half)
-                half_list = offsets[:, h * half // GROUP : (h + 1) * half // GROUP]
-                nc.vector.tensor_tensor(larger[:, cols], values[b][:].indirect(half_list), streams[b][:, cols], ALU.max)
+            for q in range(QUARTERS):
+                cols = slice(q * quarter, (q + 1) * quarter)
+                quarter_list = offsets[:, q * quarter // GROUP : (q + 1) * quarter // GROUP]
+                nc.vector.tensor_tensor(larger[:, cols], values[b][:].indirect(quarter_list), streams[b][:, cols], ALU.max)
+            product = streams[b][:, quarter:]
             for h in range(HALVES):
                 cols = slice(h * half, (h + 1) * half)
                 nc.vector.tensor_tensor(product[:, cols], larger[:, cols], gated[:, cols], ALU.mult)

import concourse.mybir as mybir

F32, U16 = mybir.dt.float32, mybir.dt.uint16
ALU = mybir.AluOpType
SILU = mybir.ActivationFunctionType.Silu
P = 128
GROUP = 16
HALVES = 2
QUARTERS = 4


def tile_lookup_vg_maxsilu_out_kernel(tc, tab, y, offs, out):
    nc = tc.nc
    rows, places = tab.shape[1], tab.shape[2]
    picks = y.shape[1]
    blocks = rows // P
    half, quarter = picks // HALVES, picks // QUARTERS

    with tc.tile_pool(name="held", bufs=1) as held:
        offsets = held.tile([P, picks // GROUP], U16, name="offsets")

        gates, values, streams = [], [], []
        for b in range(blocks):
            block_rows = slice(b * P, (b + 1) * P)
            gates.append(held.tile([P, places], F32, name=f"gates{b}"))
            values.append(held.tile([P, places], F32, name=f"values{b}"))
            streams.append(held.tile([P, picks + quarter], F32, name=f"stream{b}"))
            nc.sync.dma_start(gates[b][:], tab[1, block_rows, :])
            if b == 0:
                nc.sync.dma_start(offsets[:], offs)
            nc.sync.dma_start(streams[b][:, :half], y[block_rows, :half])
            nc.sync.dma_start(values[b][:], tab[0, block_rows, :])
            nc.sync.dma_start(streams[b][:, half:picks], y[block_rows, half:])

        for b in range(blocks):
            block_rows = slice(b * P, (b + 1) * P)
            gated = held.tile([P, picks], F32, name=f"gated{b}")
            larger = held.tile([P, picks], F32, name=f"larger{b}")
            nc.scalar.activation(gated[:], gates[b][:].indirect(offsets[:]), SILU)
            for q in range(QUARTERS):
                cols = slice(q * quarter, (q + 1) * quarter)
                quarter_list = offsets[:, q * quarter // GROUP : (q + 1) * quarter // GROUP]
                nc.vector.tensor_tensor(larger[:, cols], values[b][:].indirect(quarter_list), streams[b][:, cols], ALU.max)
            product = streams[b][:, quarter:]
            for h in range(HALVES):
                cols = slice(h * half, (h + 1) * half)
                nc.vector.tensor_tensor(product[:, cols], larger[:, cols], gated[:, cols], ALU.mult)
                nc.sync.dma_start(out[block_rows, cols], product[:, cols])
